import numpy as np
import ml_dtypes


def mxq(x, axis, fmt="e4m3"):
    dtype, down = {"e4m3": (ml_dtypes.float8_e4m3fn, 7), "e5m2": (ml_dtypes.float8_e5m2, 14)}[fmt]
    v = np.moveaxis(np.asarray(x, np.float32).astype(ml_dtypes.bfloat16).astype(np.float64), axis, -1)
    blocks = v.reshape(v.shape[:-1] + (-1, 32))
    amax = np.abs(blocks).max(-1, keepdims=True)
    byte = np.maximum(np.where(amax > 0, np.frexp(amax)[1] - 1 + 127, 0) - down, 1)
    scale = np.exp2(byte - 127.0)
    codes = (blocks / scale).astype(np.float32).astype(dtype).astype(np.float64)
    return np.moveaxis((codes * scale).reshape(v.shape), -1, axis)


WIDE = False


def mx_kscale(k):
    if not WIDE:
        return np.ones(k)
    levels = np.array([10, -10, 5, -5, 0])
    if k % 512:
        return np.exp2(np.random.permutation(np.resize(levels, k // 32))).repeat(32)
    a = np.empty((k // 512, 16))
    for p in range(k // 512):
        a[p, :8] = np.random.permutation(np.resize(levels, 8))
        for g in range(8):
            far = levels[np.abs(levels - a[p, g]) >= 10]
            a[p, g + 8] = far[np.random.randint(len(far))]
    return np.exp2(a.ravel()).repeat(32)


def f64(x):
    return np.asarray(x).astype(np.float64)


def striped8(idx):
    return np.asarray(idx).reshape(8, -1, 16).transpose(0, 2, 1).reshape(128, -1).astype(np.uint16)


def unstriped8(offs):
    return offs.reshape(8, 16, -1).transpose(0, 2, 1).reshape(8, -1).astype(np.int64)


def pick8(x, idx, run):
    r = np.arange(len(x))
    return x[r[:, None], idx[r % (8 * run) // run]]


E2M1 = np.array([0.0, 0.5, 1.0, 1.5, 2.0, 3.0, 4.0, 6.0, -0.0, -0.5, -1.0, -1.5, -2.0, -3.0, -4.0, -6.0])


def pack_weight(w, fmt):
    k, n = w.shape
    w = f64(np.asarray(w, np.float32).astype(ml_dtypes.bfloat16)).reshape(k // 32, 32, n)
    amax = np.abs(w).max(1)
    if fmt == "e4m3":
        byte = np.frexp(amax)[1] - 1 + 127 - 7
    else:
        mant, ex = np.frexp(amax / 6.0)
        byte = np.where(mant > 0.5, ex, ex - 1) + 127
    byte = np.clip(np.where(amax > 0, byte, 1), 1, 254)
    scaled = (w * np.exp2(127.0 - byte)[:, None, :]).reshape(k, n).astype(np.float32)
    by_word = np.ascontiguousarray(scaled.reshape(k // 512, 128, 4, n).transpose(0, 1, 3, 2))
    if fmt == "e4m3":
        words = by_word.astype(ml_dtypes.float8_e4m3fn).view(np.uint8)
    else:
        c = by_word.astype(ml_dtypes.float4_e2m1fn).view(np.uint8) & 0xF
        words = (c[..., 0::2] | (c[..., 1::2] << 4)).reshape(k // 512, 128, 2 * n)
    return np.ascontiguousarray(words), np.ascontiguousarray(byte.astype(np.uint8).reshape(k // 512, 16, n))


def unpack_weight(words, scales, fmt):
    g, _, n = scales.shape
    words = np.ascontiguousarray(words).reshape(g, 128, n, -1)
    if fmt == "e4m3":
        vals = words.view(ml_dtypes.float8_e4m3fn).astype(np.float64)
    else:
        nib = np.empty((g, 128, n, 4), np.uint8)
        nib[..., 0::2] = words & 0xF
        nib[..., 1::2] = words >> 4
        vals = E2M1[nib]
    vals = vals * np.repeat(np.exp2(scales.astype(np.float64) - 127.0), 8, axis=1)[..., None]
    return vals.transpose(0, 1, 3, 2).reshape(g * 512, n)


def sigmoid(v):
    return 1.0 / (1.0 + np.exp(-v))


D, K, T, I, Q = 512, 512, 1024, 512, 128


def setup_inputs():
    n = np.random.standard_normal
    idx = np.stack([np.random.permutation(T)[:I] for _ in range(8)])
    idx2 = np.stack([np.random.permutation(T)[:I] for _ in range(8)])
    idx3 = np.stack([np.random.permutation(T)[:I] for _ in range(8)])
    idx4 = np.stack([np.random.permutation(T)[:I] for _ in range(8)])
    fd = mx_kscale(D)
    fk = mx_kscale(K)
    wqp = pack_weight(n((D, K)) * 1.0 / np.sqrt(D) * fd[:, None] * fk, "e4m3")
    keysp = pack_weight(n((K, T)) * 1.0 / np.sqrt(K) / fk[:, None], "e2m1")
    tagsp = pack_weight(n((D, T)) * 0.5 / np.sqrt(D) * fd[:, None], "e4m3")
    return {
        "states": (n((D, Q)) * 0.95 / fd[:, None]).astype(np.float32),
        "wq_words": wqp[0],
        "wq_scales": wqp[1],
        "keys_words": keysp[0],
        "keys_scales": keysp[1],
        "tags_words": tagsp[0],
        "tags_scales": tagsp[1],
        "thr": (np.random.uniform(-0.6, 0.6, (Q, 1))).astype(np.float32),
        "slope": (np.random.uniform(1.0, 3.0, (Q, 1))).astype(np.float32),
        "offs": striped8(idx),
        "offs2": striped8(idx2),
        "offs3": striped8(idx3),
        "offs4": striped8(idx4),
    }


def reference(states, wq_words, wq_scales, keys_words, keys_scales, tags_words, tags_scales, thr, slope, offs, offs2, offs3, offs4):
    idx = unstriped8(offs)
    idx2 = unstriped8(offs2)
    idx3 = unstriped8(offs3)
    idx4 = unstriped8(offs4)
    wqu = unpack_weight(wq_words, wq_scales, "e4m3")
    keysu = unpack_weight(keys_words, keys_scales, "e2m1")
    tagsu = unpack_weight(tags_words, tags_scales, "e4m3")
    statesq = mxq(f64(states), 0, "e4m3")
    qv = wqu.T @ statesq
    qvq = mxq(qv, 0, "e4m3")
    a = qvq.T @ keysu + statesq.T @ tagsu
    s1 = sigmoid(pick8(a, idx, 16) * f64(slope) + f64(thr))
    w = pick8(a, idx3, 16) * s1
    f1 = np.zeros((Q, T))
    f1[np.arange(Q)[:, None], idx2[np.arange(Q) % 128 // 16]] = w
    cc = a + f1
    y = pick8(cc, idx4, 16)
    return y

@@ -1,0 +1,177 @@
+from contextlib import ExitStack
+
+import concourse.mybir as mybir
+
+D, K, T, I, Q = 512, 512, 1024, 512, 128
+FLOPS = 2 * D * K * Q + 2 * K * Q * T + 2 * D * Q * T
+
+F32 = mybir.dt.float32
+BF16 = mybir.dt.bfloat16
+I32 = mybir.dt.int32
+U32 = mybir.dt.uint32
+U16 = mybir.dt.uint16
+U8 = mybir.dt.uint8
+FP8X4 = mybir.dt.float8_e4m3fn_x4
+FP4X4 = mybir.dt.float4_e2m1fn_x4
+ACT = mybir.ActivationFunctionType
+ALU = mybir.AluOpType
+
+P = 128
+PACK = 4
+QUADRANTS = 4
+GROUP = 16
+SCORE_COLS = 256
+HALF = I // 2
+
+
+def load_scale_rows(queue, plane, scales, quadrant):
+    rows = scales[0, PACK * quadrant : PACK * (quadrant + 1), :]
+    queue.dma_start(out=plane[32 * quadrant : 32 * quadrant + PACK, :].bitcast(I32), in_=rows.bitcast(I32))
+
+
+def round_and_quantize(nc, source, rounded, codes, plane):
+    row_halves = [slice(h * Q // 2, (h + 1) * Q // 2) for h in range(2)]
+    for rows in row_halves:
+        nc.vector.tensor_copy(
+            out=rounded[:, PACK * rows.start : PACK * rows.stop].rearrange("p (q j) -> p q j", j=PACK),
+            in_=source[:, :, rows].rearrange("p j q -> p q j"),
+        )
+    for rows in row_halves:
+        nc.vector.quantize_mx(
+            out=codes[:, rows].bitcast(FP8X4), scales=plane[:, rows], in_=rounded[:, PACK * rows.start : PACK * rows.stop]
+        )
+
+
+def tile_attend_gatedhop_madeparts_kernel(
+    tc, states, wq_words, wq_scales, keys_words, keys_scales, tags_words, tags_scales, thr, slope, offs, offs2, offs3, offs4, out
+):
+    nc = tc.nc
+    with ExitStack() as ctx:
+        sb = ctx.enter_context(tc.tile_pool(name="sb", bufs=1))
+        ps = ctx.enter_context(tc.psum_pool(name="ps", bufs=1))
+
+        warm_in = sb.tile([P, 1], F32)
+        warm_out = sb.tile([P, 1], F32)
+        nc.gpsimd.memset(warm_in[:], 0.0)
+        nc.scalar.activation(warm_out[:], warm_in[:], ACT.Sigmoid)
+
+        wq_plane_raw = sb.tile([P, K], U8, align_bytes=64)
+        keys_plane = sb.tile([P, T], U8, align_bytes=64)
+        tags_plane = sb.tile([P, T], U8, align_bytes=64)
+        f1 = sb.tile([P, T], F32, align_bytes=64)
+        nc.vector.memset(wq_plane_raw[:].bitcast(I32), 0)
+        nc.vector.memset(keys_plane[:].bitcast(I32), 0)
+        nc.vector.memset(tags_plane[:].bitcast(I32), 0)
+        nc.vector.memset(f1[:], 0.0)
+
+        states_raw = sb.tile([P, PACK, Q], F32, align_bytes=64)
+        wq_codes_raw = sb.tile([P, K], U32, align_bytes=64)
+        keys_codes = sb.tile([P, 2 * T], U8, align_bytes=64)
+        tags_codes = sb.tile([P, T], U32, align_bytes=64)
+        thr_col = sb.tile([P, 1], F32)
+        slope_col = sb.tile([P, 1], F32)
+        gate_list = sb.tile([P, I // GROUP], U16)
+        place_list = sb.tile([P, I // GROUP], U16)
+        pass_list = sb.tile([P, I // GROUP], U16)
+        out_list = sb.tile([P, I // GROUP], U16)
+
+        nc.sync.dma_start(out=states_raw[:], in_=states.rearrange("(p j) q -> p j q", j=PACK))
+        for quadrant in range(QUADRANTS):
+            load_scale_rows(nc.sync, wq_plane_raw, wq_scales, quadrant)
+        nc.sync.dma_start(out=wq_codes_raw[:].bitcast(I32), in_=wq_words[0].rearrange("p n t -> p (n t)").bitcast(I32))
+        nc.sync.dma_start(out=keys_codes[:].bitcast(I32), in_=keys_words[0].bitcast(I32))
+        load_scale_rows(nc.sync, keys_plane, keys_scales, 0)
+        nc.sync.dma_start(out=tags_codes[:].bitcast(I32), in_=tags_words[0].rearrange("p n t -> p (n t)").bitcast(I32))
+        for quadrant in range(QUADRANTS):
+            load_scale_rows(nc.sync, tags_plane, tags_scales, quadrant)
+        for quadrant in range(1, QUADRANTS):
+            load_scale_rows(nc.sync, keys_plane, keys_scales, quadrant)
+        nc.sync.dma_start(gate_list[:], offs)
+        nc.sync.dma_start(pass_list[:], offs3)
+        nc.sync.dma_start(place_list[:], offs2)
+        nc.sync.dma_start(out_list[:], offs4)
+        nc.gpsimd.dma_start(out=slope_col[:], in_=slope)
+        nc.gpsimd.dma_start(out=thr_col[:], in_=thr)
+
+        wq_plane = sb.tile([P, K], U8, align_bytes=64)
+        wq_codes = sb.tile([P, K], U32, align_bytes=64)
+        nc.vector.tensor_copy(
+            out=wq_plane[:].rearrange("p (j m) -> p m j", j=PACK), in_=wq_plane_raw[:].rearrange("p (m j) -> p m j", j=PACK)
+        )
+        nc.scalar.copy(
+            out=wq_codes[:].rearrange("p (j m) -> p m j", j=PACK), in_=wq_codes_raw[:].rearrange("p (m j) -> p m j", j=PACK)
+        )
+
+        states_bf = sb.tile([P, Q * PACK], BF16, align_bytes=64)
+        states_codes = sb.tile([P, Q], U32, align_bytes=64)
+        states_plane = sb.tile([P, Q], U8, align_bytes=64)
+        round_and_quantize(nc, states_raw, states_bf, states_codes, states_plane)
+
+        qv_bank = ps.tile([P, PACK, Q], F32)
+        for j in range(PACK):
+            cols = slice(P * j, P * (j + 1))
+            nc.tensor.matmul_mx(
+                out=qv_bank[:, j, :],
+                lhsT=wq_codes[:, cols].bitcast(FP8X4),
+                lhsT_scale=wq_plane[:, cols],
+                rhs=states_codes[:].bitcast(FP8X4),
+                rhs_scale=states_plane[:],
+                start=True,
+                stop=True,
+            )
+
+        banks = [ps.tile([P, SCORE_COLS], F32, name=f"score_bank{b}") for b in range(T // SCORE_COLS)]
+        for b, bank in enumerate(banks):
+            cols = slice(SCORE_COLS * b, SCORE_COLS * (b + 1))
+            nc.tensor.matmul_mx(
+                out=bank[:],
+                lhsT=states_codes[:].bitcast(FP8X4),
+                lhsT_scale=states_plane[:],
+                rhs=tags_codes[:, cols].bitcast(FP8X4),
+                rhs_scale=tags_plane[:, cols],
+                start=True,
+                stop=False,
+            )
+
+        qv_bf = sb.tile([P, Q * PACK], BF16, align_bytes=64)
+        qv_codes = sb.tile([P, Q], U32, align_bytes=64)
+        qv_plane = sb.tile([P, Q], U8, align_bytes=64)
+        round_and_quantize(nc, qv_bank, qv_bf, qv_codes, qv_plane)
+
+        a = sb.tile([P, T], F32, align_bytes=64)
+        for b, bank in enumerate(banks):
+            cols = slice(SCORE_COLS * b, SCORE_COLS * (b + 1))
+            nc.tensor.matmul_mx(
+                out=bank[:],
+                lhsT=qv_codes[:].bitcast(FP8X4),
+                lhsT_scale=qv_plane[:],
+                rhs=keys_codes[:, 2 * cols.start : 2 * cols.stop].bitcast(FP4X4),
+                rhs_scale=keys_plane[:, cols],
+                start=False,
+                stop=True,
+            )
+            if b % 2 == 0:
+                nc.scalar.copy(out=a[:, cols], in_=bank[:])
+            else:
+                nc.vector.tensor_copy(out=a[:, cols], in_=bank[:])
+
+        halves = [slice(h * HALF // GROUP, (h + 1) * HALF // GROUP) for h in range(2)]
+        gates = [sb.tile([P, HALF], F32, name=f"gate{h}") for h in range(2)]
+        passed = [sb.tile([P, HALF], F32, name=f"passed{h}") for h in range(2)]
+        nc.vector.tensor_copy(passed[0][:], a[:].indirect(pass_list[:, halves[0]]))
+        for h in range(2):
+            nc.scalar.activation(
+                gates[h][:], a[:].indirect(gate_list[:, halves[h]]), ACT.Sigmoid, bias=thr_col[:], scale=slope_col[:]
+            )
+        nc.scalar.activation(passed[1][:], a[:].indirect(pass_list[:, halves[1]]), ACT.Copy)
+        for h in range(2):
+            nc.vector.tensor_tensor(f1[:].indirect(place_list[:, halves[h]]), passed[h][:], gates[h][:], ALU.mult)
+
+        cc = sb.tile([P, T], F32, align_bytes=64)
+        nc.vector.tensor_tensor(cc[:], a[:], f1[:], ALU.add)
+
+        results = [sb.tile([P, HALF], F32, name=f"result{h}") for h in range(2)]
+        nc.vector.tensor_copy(results[0][:], cc[:].indirect(out_list[:, halves[0]]))
+        nc.scalar.activation(results[1][:], cc[:].indirect(out_list[:, halves[1]]), ACT.Copy)
+        nc.sync.dma_start(out=out[:, 0:HALF], in_=results[0][:])
+        nc.scalar.dma_start(out=out[:, HALF:I], in_=results[1][:])

@@ -22,6 +22,8 @@ QUADRANTS = 4
 GROUP = 16
 SCORE_COLS = 256
 HALF = I // 2
+DEAL_ON_SCALAR = 48
+ADD_ON_VECTOR = 704
 
 
 def load_scale_rows(queue, plane, scales, quadrant):
@@ -29,10 +31,10 @@ def load_scale_rows(queue, plane, scales, quadrant):
     queue.dma_start(out=plane[32 * quadrant : 32 * quadrant + PACK, :].bitcast(I32), in_=rows.bitcast(I32))
 
 
-def round_and_quantize(nc, source, rounded, codes, plane):
+def round_and_quantize(nc, copies, source, rounded, codes, plane):
     row_halves = [slice(h * Q // 2, (h + 1) * Q // 2) for h in range(2)]
-    for rows in row_halves:
-        nc.vector.tensor_copy(
+    for copy, rows in zip(copies, row_halves):
+        copy(
             out=rounded[:, PACK * rows.start : PACK * rows.stop].rearrange("p (q j) -> p q j", j=PACK),
             in_=source[:, :, rows].rearrange("p j q -> p q j"),
         )
@@ -60,15 +62,15 @@ def tile_attend_gatedhop_madeparts_kernel(
         tags_plane = sb.tile([P, T], U8, align_bytes=64)
         f1 = sb.tile([P, T], F32, align_bytes=64)
         nc.vector.memset(wq_plane_raw[:].bitcast(I32), 0)
-        nc.vector.memset(keys_plane[:].bitcast(I32), 0)
         nc.vector.memset(tags_plane[:].bitcast(I32), 0)
+        nc.vector.memset(keys_plane[:].bitcast(I32), 0)
         nc.vector.memset(f1[:], 0.0)
 
         states_raw = sb.tile([P, PACK, Q], F32, align_bytes=64)
         wq_codes_raw = sb.tile([P, K], U32, align_bytes=64)
         keys_codes = sb.tile([P, 2 * T], U8, align_bytes=64)
         tags_codes = sb.tile([P, T], U32, align_bytes=64)
-        thr_col = sb.tile([P, 1], F32)
+        thr_col = sb.tile([P, 1], F32, tag="thr_then_passed")
         slope_col = sb.tile([P, 1], F32)
         gate_list = sb.tile([P, I // GROUP], U16)
         place_list = sb.tile([P, I // GROUP], U16)
@@ -79,33 +81,33 @@ def tile_attend_gatedhop_madeparts_kernel(
         for quadrant in range(QUADRANTS):
             load_scale_rows(nc.sync, wq_plane_raw, wq_scales, quadrant)
         nc.sync.dma_start(out=wq_codes_raw[:].bitcast(I32), in_=wq_words[0].rearrange("p n t -> p (n t)").bitcast(I32))
-        nc.sync.dma_start(out=keys_codes[:].bitcast(I32), in_=keys_words[0].bitcast(I32))
-        load_scale_rows(nc.sync, keys_plane, keys_scales, 0)
         nc.sync.dma_start(out=tags_codes[:].bitcast(I32), in_=tags_words[0].rearrange("p n t -> p (n t)").bitcast(I32))
         for quadrant in range(QUADRANTS):
             load_scale_rows(nc.sync, tags_plane, tags_scales, quadrant)
-        for quadrant in range(1, QUADRANTS):
-            load_scale_rows(nc.sync, keys_plane, keys_scales, quadrant)
+        nc.sync.dma_start(out=keys_codes[:].bitcast(I32), in_=keys_words[0].bitcast(I32))
+        for quadrant in range(QUADRANTS):
+            load_scale_rows(nc.sync if quadrant < 2 else nc.gpsimd, keys_plane, keys_scales, quadrant)
+        nc.sync.dma_start(out=slope_col[:], in_=slope)
+        nc.sync.dma_start(out=thr_col[:], in_=thr)
         nc.sync.dma_start(gate_list[:], offs)
         nc.sync.dma_start(pass_list[:], offs3)
         nc.sync.dma_start(place_list[:], offs2)
         nc.sync.dma_start(out_list[:], offs4)
-        nc.gpsimd.dma_start(out=slope_col[:], in_=slope)
-        nc.gpsimd.dma_start(out=thr_col[:], in_=thr)
 
         wq_plane = sb.tile([P, K], U8, align_bytes=64)
         wq_codes = sb.tile([P, K], U32, align_bytes=64)
         nc.vector.tensor_copy(
             out=wq_plane[:].rearrange("p (j m) -> p m j", j=PACK), in_=wq_plane_raw[:].rearrange("p (m j) -> p m j", j=PACK)
         )
-        nc.scalar.copy(
-            out=wq_codes[:].rearrange("p (j m) -> p m j", j=PACK), in_=wq_codes_raw[:].rearrange("p (m j) -> p m j", j=PACK)
-        )
+        dealt = wq_codes[:].rearrange("p (j m) -> p m j", j=PACK)
+        undealt = wq_codes_raw[:].rearrange("p (m j) -> p m j", j=PACK)
 
         states_bf = sb.tile([P, Q * PACK], BF16, align_bytes=64)
         states_codes = sb.tile([P, Q], U32, align_bytes=64)
         states_plane = sb.tile([P, Q], U8, align_bytes=64)
-        round_and_quantize(nc, states_raw, states_bf, states_codes, states_plane)
+        round_and_quantize(nc, (nc.vector.tensor_copy, nc.scalar.copy), states_raw, states_bf, states_codes, states_plane)
+        nc.scalar.copy(out=dealt[:, :DEAL_ON_SCALAR, :], in_=undealt[:, :DEAL_ON_SCALAR, :])
+        nc.vector.tensor_copy(out=dealt[:, DEAL_ON_SCALAR:, :].bitcast(I32), in_=undealt[:, DEAL_ON_SCALAR:, :].bitcast(I32))
 
         qv_bank = ps.tile([P, PACK, Q], F32)
         for j in range(PACK):
@@ -136,7 +138,7 @@ def tile_attend_gatedhop_madeparts_kernel(
         qv_bf = sb.tile([P, Q * PACK], BF16, align_bytes=64)
         qv_codes = sb.tile([P, Q], U32, align_bytes=64)
         qv_plane = sb.tile([P, Q], U8, align_bytes=64)
-        round_and_quantize(nc, qv_bank, qv_bf, qv_codes, qv_plane)
+        round_and_quantize(nc, (nc.vector.tensor_copy, nc.vector.tensor_copy), qv_bank, qv_bf, qv_codes, qv_plane)
 
         a = sb.tile([P, T], F32, align_bytes=64)
         for b, bank in enumerate(banks):
@@ -157,18 +159,23 @@ def tile_attend_gatedhop_madeparts_kernel(
 
         halves = [slice(h * HALF // GROUP, (h + 1) * HALF // GROUP) for h in range(2)]
         gates = [sb.tile([P, HALF], F32, name=f"gate{h}") for h in range(2)]
-        passed = [sb.tile([P, HALF], F32, name=f"passed{h}") for h in range(2)]
+        passed = [sb.tile([P, HALF], F32, name="passed0")]
         nc.vector.tensor_copy(passed[0][:], a[:].indirect(pass_list[:, halves[0]]))
         for h in range(2):
             nc.scalar.activation(
                 gates[h][:], a[:].indirect(gate_list[:, halves[h]]), ACT.Sigmoid, bias=thr_col[:], scale=slope_col[:]
             )
+        passed.append(sb.tile([P, HALF], F32, name="passed1", tag="thr_then_passed"))
         nc.scalar.activation(passed[1][:], a[:].indirect(pass_list[:, halves[1]]), ACT.Copy)
         for h in range(2):
             nc.vector.tensor_tensor(f1[:].indirect(place_list[:, halves[h]]), passed[h][:], gates[h][:], ALU.mult)
 
         cc = sb.tile([P, T], F32, align_bytes=64)
-        nc.vector.tensor_tensor(cc[:], a[:], f1[:], ALU.add)
+        nc.gpsimd.tensor_tensor(cc[:, ADD_ON_VECTOR:], a[:, ADD_ON_VECTOR:], f1[:, ADD_ON_VECTOR:], ALU.add)
+        for first in range(0, ADD_ON_VECTOR, SCORE_COLS):
+            width = min(SCORE_COLS, ADD_ON_VECTOR - first)
+            cols = slice(first, first + width)
+            nc.vector.tensor_tensor(cc[:, cols], banks[first // SCORE_COLS][:, :width], f1[:, cols], ALU.add)
 
         results = [sb.tile([P, HALF], F32, name=f"result{h}") for h in range(2)]
         nc.vector.tensor_copy(results[0][:], cc[:].indirect(out_list[:, halves[0]]))

@@ -22,8 +22,8 @@ QUADRANTS = 4
 GROUP = 16
 SCORE_COLS = 256
 HALF = I // 2
-DEAL_ON_SCALAR = 48
-ADD_ON_VECTOR = 704
+DEAL_ON_SCALAR = 72
+ADD_ON_VECTOR = 672
 
 
 def load_scale_rows(queue, plane, scales, quadrant):
@@ -78,9 +78,11 @@ def tile_attend_gatedhop_madeparts_kernel(
         out_list = sb.tile([P, I // GROUP], U16)
 
         nc.sync.dma_start(out=states_raw[:], in_=states.rearrange("(p j) q -> p j q", j=PACK))
-        for quadrant in range(QUADRANTS):
+        for quadrant in range(2):
             load_scale_rows(nc.sync, wq_plane_raw, wq_scales, quadrant)
         nc.sync.dma_start(out=wq_codes_raw[:].bitcast(I32), in_=wq_words[0].rearrange("p n t -> p (n t)").bitcast(I32))
+        for quadrant in range(2, QUADRANTS):
+            load_scale_rows(nc.sync, wq_plane_raw, wq_scales, quadrant)
         nc.sync.dma_start(out=tags_codes[:].bitcast(I32), in_=tags_words[0].rearrange("p n t -> p (n t)").bitcast(I32))
         for quadrant in range(QUADRANTS):
             load_scale_rows(nc.sync, tags_plane, tags_scales, quadrant)
@@ -109,11 +111,11 @@ def tile_attend_gatedhop_madeparts_kernel(
         nc.scalar.copy(out=dealt[:, :DEAL_ON_SCALAR, :], in_=undealt[:, :DEAL_ON_SCALAR, :])
         nc.vector.tensor_copy(out=dealt[:, DEAL_ON_SCALAR:, :].bitcast(I32), in_=undealt[:, DEAL_ON_SCALAR:, :].bitcast(I32))
 
-        qv_bank = ps.tile([P, PACK, Q], F32)
+        qv_banks = [ps.tile([P, 2, Q], F32, name=f"qv_bank{u}") for u in range(2)]
         for j in range(PACK):
             cols = slice(P * j, P * (j + 1))
             nc.tensor.matmul_mx(
-                out=qv_bank[:, j, :],
+                out=qv_banks[j // 2][:, j % 2, :],
                 lhsT=wq_codes[:, cols].bitcast(FP8X4),
                 lhsT_scale=wq_plane[:, cols],
                 rhs=states_codes[:].bitcast(FP8X4),
@@ -138,7 +140,10 @@ def tile_attend_gatedhop_madeparts_kernel(
         qv_bf = sb.tile([P, Q * PACK], BF16, align_bytes=64)
         qv_codes = sb.tile([P, Q], U32, align_bytes=64)
         qv_plane = sb.tile([P, Q], U8, align_bytes=64)
-        round_and_quantize(nc, (nc.vector.tensor_copy, nc.vector.tensor_copy), qv_bank, qv_bf, qv_codes, qv_plane)
+        qv_places = qv_bf[:].rearrange("p (q j) -> p q j", j=PACK)
+        nc.vector.tensor_copy(out=qv_places[:, :, 0:2], in_=qv_banks[0][:].rearrange("p j q -> p q j"))
+        nc.scalar.copy(out=qv_places[:, :, 2:4], in_=qv_banks[1][:].rearrange("p j q -> p q j"))
+        nc.vector.quantize_mx(out=qv_codes[:].bitcast(FP8X4), scales=qv_plane[:], in_=qv_bf[:])
 
         a = sb.tile([P, T], F32, align_bytes=64)
         for b, bank in enumerate(banks):

@@ -17,31 +17,22 @@ ACT = mybir.ActivationFunctionType
 ALU = mybir.AluOpType
 
 P = 128
-PACK = 4
+PLACES = 4
 QUADRANTS = 4
-GROUP = 16
-SCORE_COLS = 256
+QUADRANT_ROWS = 32
+SCALE_ROWS = 4
+HEAD_ROWS = 16
 HALF = I // 2
+
+SCORE_EDGES = (0, 256, 512, 768, 896, 1024)
 DEAL_ON_SCALAR = 72
 ADD_ON_VECTOR = 672
 
 
 def load_scale_rows(queue, plane, scales, quadrant):
-    rows = scales[0, PACK * quadrant : PACK * (quadrant + 1), :]
-    queue.dma_start(out=plane[32 * quadrant : 32 * quadrant + PACK, :].bitcast(I32), in_=rows.bitcast(I32))
-
-
-def round_and_quantize(nc, copies, source, rounded, codes, plane):
-    row_halves = [slice(h * Q // 2, (h + 1) * Q // 2) for h in range(2)]
-    for copy, rows in zip(copies, row_halves):
-        copy(
-            out=rounded[:, PACK * rows.start : PACK * rows.stop].rearrange("p (q j) -> p q j", j=PACK),
-            in_=source[:, :, rows].rearrange("p j q -> p q j"),
-        )
-    for rows in row_halves:
-        nc.vector.quantize_mx(
-            out=codes[:, rows].bitcast(FP8X4), scales=plane[:, rows], in_=rounded[:, PACK * rows.start : PACK * rows.stop]
-        )
+    rows = scales[0, SCALE_ROWS * quadrant : SCALE_ROWS * (quadrant + 1), :]
+    first = QUADRANT_ROWS * quadrant
+    queue.dma_start(out=plane[first : first + SCALE_ROWS, :].bitcast(I32), in_=rows.bitcast(I32))
 
 
 def tile_attend_gatedhop_madeparts_kernel(
@@ -66,31 +57,33 @@ def tile_attend_gatedhop_madeparts_kernel(
         nc.vector.memset(keys_plane[:].bitcast(I32), 0)
         nc.vector.memset(f1[:], 0.0)
 
-        states_raw = sb.tile([P, PACK, Q], F32, align_bytes=64)
+        states_raw = sb.tile([P, PLACES, Q], F32, align_bytes=64)
         wq_codes_raw = sb.tile([P, K], U32, align_bytes=64)
         keys_codes = sb.tile([P, 2 * T], U8, align_bytes=64)
         tags_codes = sb.tile([P, T], U32, align_bytes=64)
         thr_col = sb.tile([P, 1], F32, tag="thr_then_passed")
         slope_col = sb.tile([P, 1], F32)
-        gate_list = sb.tile([P, I // GROUP], U16)
-        place_list = sb.tile([P, I // GROUP], U16)
-        pass_list = sb.tile([P, I // GROUP], U16)
-        out_list = sb.tile([P, I // GROUP], U16)
+        gate_list = sb.tile([P, I // HEAD_ROWS], U16)
+        place_list = sb.tile([P, I // HEAD_ROWS], U16)
+        pass_list = sb.tile([P, I // HEAD_ROWS], U16)
+        out_list = sb.tile([P, I // HEAD_ROWS], U16)
 
-        nc.sync.dma_start(out=states_raw[:], in_=states.rearrange("(p j) q -> p j q", j=PACK))
-        for quadrant in range(2):
+        nc.sync.dma_start(out=states_raw[:], in_=states.rearrange("(p j) q -> p j q", j=PLACES))
+        for quadrant in range(QUADRANTS // 2):
             load_scale_rows(nc.sync, wq_plane_raw, wq_scales, quadrant)
         nc.sync.dma_start(out=wq_codes_raw[:].bitcast(I32), in_=wq_words[0].rearrange("p n t -> p (n t)").bitcast(I32))
-        for quadrant in range(2, QUADRANTS):
+        for quadrant in range(QUADRANTS // 2, QUADRANTS):
             load_scale_rows(nc.sync, wq_plane_raw, wq_scales, quadrant)
+        load_scale_rows(nc.sync, tags_plane, tags_scales, 0)
         nc.sync.dma_start(out=tags_codes[:].bitcast(I32), in_=tags_words[0].rearrange("p n t -> p (n t)").bitcast(I32))
-        for quadrant in range(QUADRANTS):
+        for quadrant in range(1, QUADRANTS):
             load_scale_rows(nc.sync, tags_plane, tags_scales, quadrant)
         nc.sync.dma_start(out=keys_codes[:].bitcast(I32), in_=keys_words[0].bitcast(I32))
-        for quadrant in range(QUADRANTS):
-            load_scale_rows(nc.sync if quadrant < 2 else nc.gpsimd, keys_plane, keys_scales, quadrant)
+        nc.gpsimd.dma_start(out=thr_col[:], in_=thr)
+        for quadrant in range(QUADRANTS - 1):
+            load_scale_rows(nc.sync, keys_plane, keys_scales, quadrant)
+        load_scale_rows(nc.gpsimd, keys_plane, keys_scales, QUADRANTS - 1)
         nc.sync.dma_start(out=slope_col[:], in_=slope)
-        nc.sync.dma_start(out=thr_col[:], in_=thr)
         nc.sync.dma_start(gate_list[:], offs)
         nc.sync.dma_start(pass_list[:], offs3)
         nc.sync.dma_start(place_list[:], offs2)
@@ -99,20 +92,32 @@ def tile_attend_gatedhop_madeparts_kernel(
         wq_plane = sb.tile([P, K], U8, align_bytes=64)
         wq_codes = sb.tile([P, K], U32, align_bytes=64)
         nc.vector.tensor_copy(
-            out=wq_plane[:].rearrange("p (j m) -> p m j", j=PACK), in_=wq_plane_raw[:].rearrange("p (m j) -> p m j", j=PACK)
+            out=wq_plane[:].rearrange("p (j m) -> p m j", j=PLACES), in_=wq_plane_raw[:].rearrange("p (m j) -> p m j", j=PLACES)
         )
-        dealt = wq_codes[:].rearrange("p (j m) -> p m j", j=PACK)
-        undealt = wq_codes_raw[:].rearrange("p (m j) -> p m j", j=PACK)
+        dealt = wq_codes[:].rearrange("p (j m) -> p m j", j=PLACES)
+        undealt = wq_codes_raw[:].rearrange("p (m j) -> p m j", j=PLACES)
 
-        states_bf = sb.tile([P, Q * PACK], BF16, align_bytes=64)
+        states_bf = sb.tile([P, Q * PLACES], BF16, align_bytes=64)
         states_codes = sb.tile([P, Q], U32, align_bytes=64)
         states_plane = sb.tile([P, Q], U8, align_bytes=64)
-        round_and_quantize(nc, (nc.vector.tensor_copy, nc.scalar.copy), states_raw, states_bf, states_codes, states_plane)
+        row_halves = [slice(h * Q // 2, (h + 1) * Q // 2) for h in range(2)]
+        for engine_copy, rows in zip((nc.vector.tensor_copy, nc.scalar.copy), row_halves):
+            engine_copy(
+                out=states_bf[:, PLACES * rows.start : PLACES * rows.stop].rearrange("p (q j) -> p q j", j=PLACES),
+                in_=states_raw[:, :, rows].rearrange("p j q -> p q j"),
+            )
+        for rows in row_halves:
+            nc.vector.quantize_mx(
+                out=states_codes[:, rows].bitcast(FP8X4),
+                scales=states_plane[:, rows],
+                in_=states_bf[:, PLACES * rows.start : PLACES * rows.stop],
+            )
+
         nc.scalar.copy(out=dealt[:, :DEAL_ON_SCALAR, :], in_=undealt[:, :DEAL_ON_SCALAR, :])
         nc.vector.tensor_copy(out=dealt[:, DEAL_ON_SCALAR:, :].bitcast(I32), in_=undealt[:, DEAL_ON_SCALAR:, :].bitcast(I32))
 
-        qv_banks = [ps.tile([P, 2, Q], F32, name=f"qv_bank{u}") for u in range(2)]
-        for j in range(PACK):
+        qv_banks = [ps.tile([P, 2, Q], F32, name=f"qv_bank{pair}") for pair in range(PLACES // 2)]
+        for j in range(PLACES):
             cols = slice(P * j, P * (j + 1))
             nc.tensor.matmul_mx(
                 out=qv_banks[j // 2][:, j % 2, :],
@@ -124,9 +129,9 @@ def tile_attend_gatedhop_madeparts_kernel(
                 stop=True,
             )
 
-        banks = [ps.tile([P, SCORE_COLS], F32, name=f"score_bank{b}") for b in range(T // SCORE_COLS)]
-        for b, bank in enumerate(banks):
-            cols = slice(SCORE_COLS * b, SCORE_COLS * (b + 1))
+        spans = [slice(first, last) for first, last in zip(SCORE_EDGES, SCORE_EDGES[1:])]
+        banks = [ps.tile([P, cols.stop - cols.start], F32, name=f"score_bank{cols.start}") for cols in spans]
+        for cols, bank in zip(spans, banks):
             nc.tensor.matmul_mx(
                 out=bank[:],
                 lhsT=states_codes[:].bitcast(FP8X4),
@@ -137,17 +142,16 @@ def tile_attend_gatedhop_madeparts_kernel(
                 stop=False,
             )
 
-        qv_bf = sb.tile([P, Q * PACK], BF16, align_bytes=64)
+        qv_bf = sb.tile([P, Q * PLACES], BF16, align_bytes=64)
         qv_codes = sb.tile([P, Q], U32, align_bytes=64)
         qv_plane = sb.tile([P, Q], U8, align_bytes=64)
-        qv_places = qv_bf[:].rearrange("p (q j) -> p q j", j=PACK)
+        qv_places = qv_bf[:].rearrange("p (q j) -> p q j", j=PLACES)
         nc.vector.tensor_copy(out=qv_places[:, :, 0:2], in_=qv_banks[0][:].rearrange("p j q -> p q j"))
         nc.scalar.copy(out=qv_places[:, :, 2:4], in_=qv_banks[1][:].rearrange("p j q -> p q j"))
         nc.vector.quantize_mx(out=qv_codes[:].bitcast(FP8X4), scales=qv_plane[:], in_=qv_bf[:])
 
         a = sb.tile([P, T], F32, align_bytes=64)
-        for b, bank in enumerate(banks):
-            cols = slice(SCORE_COLS * b, SCORE_COLS * (b + 1))
+        for b, (cols, bank) in enumerate(zip(spans, banks)):
             nc.tensor.matmul_mx(
                 out=bank[:],
                 lhsT=qv_codes[:].bitcast(FP8X4),
@@ -157,33 +161,34 @@ def tile_attend_gatedhop_madeparts_kernel(
                 start=False,
                 stop=True,
             )
-            if b % 2 == 0:
+            if b % 2 == 1:
                 nc.scalar.copy(out=a[:, cols], in_=bank[:])
             else:
                 nc.vector.tensor_copy(out=a[:, cols], in_=bank[:])
 
-        halves = [slice(h * HALF // GROUP, (h + 1) * HALF // GROUP) for h in range(2)]
-        gates = [sb.tile([P, HALF], F32, name=f"gate{h}") for h in range(2)]
-        passed = [sb.tile([P, HALF], F32, name="passed0")]
-        nc.vector.tensor_copy(passed[0][:], a[:].indirect(pass_list[:, halves[0]]))
-        for h in range(2):
-            nc.scalar.activation(
-                gates[h][:], a[:].indirect(gate_list[:, halves[h]]), ACT.Sigmoid, bias=thr_col[:], scale=slope_col[:]
-            )
-        passed.append(sb.tile([P, HALF], F32, name="passed1", tag="thr_then_passed"))
-        nc.scalar.activation(passed[1][:], a[:].indirect(pass_list[:, halves[1]]), ACT.Copy)
-        for h in range(2):
-            nc.vector.tensor_tensor(f1[:].indirect(place_list[:, halves[h]]), passed[h][:], gates[h][:], ALU.mult)
+        first, second = [slice(h * HALF // HEAD_ROWS, (h + 1) * HALF // HEAD_ROWS) for h in range(2)]
+        gate_first = sb.tile([P, HALF], F32)
+        gate_second = sb.tile([P, HALF], F32)
+        passed_first = sb.tile([P, HALF], F32)
+        nc.vector.tensor_copy(passed_first[:], a[:].indirect(pass_list[:, first]))
+        for gate, half in ((gate_first, first), (gate_second, second)):
+            nc.scalar.activation(gate[:], a[:].indirect(gate_list[:, half]), ACT.Sigmoid, bias=thr_col[:], scale=slope_col[:])
+        passed_second = sb.tile([P, HALF], F32, tag="thr_then_passed")
+        nc.scalar.activation(passed_second[:], a[:].indirect(pass_list[:, second]), ACT.Copy)
+
+        for passed, gate, half in ((passed_first, gate_first, first), (passed_second, gate_second, second)):
+            nc.vector.tensor_tensor(f1[:].indirect(place_list[:, half]), passed[:], gate[:], ALU.mult)
 
         cc = sb.tile([P, T], F32, align_bytes=64)
         nc.gpsimd.tensor_tensor(cc[:, ADD_ON_VECTOR:], a[:, ADD_ON_VECTOR:], f1[:, ADD_ON_VECTOR:], ALU.add)
-        for first in range(0, ADD_ON_VECTOR, SCORE_COLS):
-            width = min(SCORE_COLS, ADD_ON_VECTOR - first)
-            cols = slice(first, first + width)
-            nc.vector.tensor_tensor(cc[:, cols], banks[first // SCORE_COLS][:, :width], f1[:, cols], ALU.add)
+        for span, bank in zip(spans, banks):
+            if span.start < ADD_ON_VECTOR:
+                cols = slice(span.start, min(span.stop, ADD_ON_VECTOR))
+                nc.vector.tensor_tensor(cc[:, cols], bank[:, : cols.stop - cols.start], f1[:, cols], ALU.add)
 
-        results = [sb.tile([P, HALF], F32, name=f"result{h}") for h in range(2)]
-        nc.vector.tensor_copy(results[0][:], cc[:].indirect(out_list[:, halves[0]]))
-        nc.scalar.activation(results[1][:], cc[:].indirect(out_list[:, halves[1]]), ACT.Copy)
-        nc.sync.dma_start(out=out[:, 0:HALF], in_=results[0][:])
-        nc.scalar.dma_start(out=out[:, HALF:I], in_=results[1][:])
+        result_first = sb.tile([P, HALF], F32)
+        result_second = sb.tile([P, HALF], F32)
+        nc.vector.tensor_copy(result_first[:], cc[:].indirect(out_list[:, first]))
+        nc.scalar.activation(result_second[:], cc[:].indirect(out_list[:, second]), ACT.Copy)
+        nc.sync.dma_start(out=out[:, :HALF], in_=result_first[:])
+        nc.scalar.dma_start(out=out[:, HALF:], in_=result_second[:])

from contextlib import ExitStack

import concourse.mybir as mybir

D, K, T, I, Q = 512, 512, 1024, 512, 128
FLOPS = 2 * D * K * Q + 2 * K * Q * T + 2 * D * Q * T

F32 = mybir.dt.float32
BF16 = mybir.dt.bfloat16
I32 = mybir.dt.int32
U32 = mybir.dt.uint32
U16 = mybir.dt.uint16
U8 = mybir.dt.uint8
FP8X4 = mybir.dt.float8_e4m3fn_x4
FP4X4 = mybir.dt.float4_e2m1fn_x4
ACT = mybir.ActivationFunctionType
ALU = mybir.AluOpType

P = 128
PLACES = 4
QUADRANTS = 4
QUADRANT_ROWS = 32
SCALE_ROWS = 4
HEAD_ROWS = 16
HALF = I // 2

SCORE_EDGES = (0, 256, 512, 768, 896, 1024)
DEAL_ON_SCALAR = 72
ADD_ON_VECTOR = 672


def load_scale_rows(queue, plane, scales, quadrant):
    rows = scales[0, SCALE_ROWS * quadrant : SCALE_ROWS * (quadrant + 1), :]
    first = QUADRANT_ROWS * quadrant
    queue.dma_start(out=plane[first : first + SCALE_ROWS, :].bitcast(I32), in_=rows.bitcast(I32))


def tile_attend_gatedhop_madeparts_kernel(
    tc, states, wq_words, wq_scales, keys_words, keys_scales, tags_words, tags_scales, thr, slope, offs, offs2, offs3, offs4, out
):
    nc = tc.nc
    with ExitStack() as ctx:
        sb = ctx.enter_context(tc.tile_pool(name="sb", bufs=1))
        ps = ctx.enter_context(tc.psum_pool(name="ps", bufs=1))

        warm_in = sb.tile([P, 1], F32)
        warm_out = sb.tile([P, 1], F32)
        nc.gpsimd.memset(warm_in[:], 0.0)
        nc.scalar.activation(warm_out[:], warm_in[:], ACT.Sigmoid)

        wq_plane_raw = sb.tile([P, K], U8, align_bytes=64)
        keys_plane = sb.tile([P, T], U8, align_bytes=64)
        tags_plane = sb.tile([P, T], U8, align_bytes=64)
        f1 = sb.tile([P, T], F32, align_bytes=64)
        nc.vector.memset(wq_plane_raw[:].bitcast(I32), 0)
        nc.vector.memset(tags_plane[:].bitcast(I32), 0)
        nc.vector.memset(keys_plane[:].bitcast(I32), 0)
        nc.vector.memset(f1[:], 0.0)

        states_raw = sb.tile([P, PLACES, Q], F32, align_bytes=64)
        wq_codes_raw = sb.tile([P, K], U32, align_bytes=64)
        keys_codes = sb.tile([P, 2 * T], U8, align_bytes=64)
        tags_codes = sb.tile([P, T], U32, align_bytes=64)
        thr_col = sb.tile([P, 1], F32, tag="thr_then_passed")
        slope_col = sb.tile([P, 1], F32)
        gate_list = sb.tile([P, I // HEAD_ROWS], U16)
        place_list = sb.tile([P, I // HEAD_ROWS], U16)
        pass_list = sb.tile([P, I // HEAD_ROWS], U16)
        out_list = sb.tile([P, I // HEAD_ROWS], U16)

        nc.sync.dma_start(out=states_raw[:], in_=states.rearrange("(p j) q -> p j q", j=PLACES))
        for quadrant in range(QUADRANTS // 2):
            load_scale_rows(nc.sync, wq_plane_raw, wq_scales, quadrant)
        nc.sync.dma_start(out=wq_codes_raw[:].bitcast(I32), in_=wq_words[0].rearrange("p n t -> p (n t)").bitcast(I32))
        for quadrant in range(QUADRANTS // 2, QUADRANTS):
            load_scale_rows(nc.sync, wq_plane_raw, wq_scales, quadrant)
        load_scale_rows(nc.sync, tags_plane, tags_scales, 0)
        nc.sync.dma_start(out=tags_codes[:].bitcast(I32), in_=tags_words[0].rearrange("p n t -> p (n t)").bitcast(I32))
        for quadrant in range(1, QUADRANTS):
            load_scale_rows(nc.sync, tags_plane, tags_scales, quadrant)
        nc.sync.dma_start(out=keys_codes[:].bitcast(I32), in_=keys_words[0].bitcast(I32))
        nc.gpsimd.dma_start(out=thr_col[:], in_=thr)
        for quadrant in range(QUADRANTS - 1):
            load_scale_rows(nc.sync, keys_plane, keys_scales, quadrant)
        load_scale_rows(nc.gpsimd, keys_plane, keys_scales, QUADRANTS - 1)
        nc.sync.dma_start(out=slope_col[:], in_=slope)
        nc.sync.dma_start(gate_list[:], offs)
        nc.sync.dma_start(pass_list[:], offs3)
        nc.sync.dma_start(place_list[:], offs2)
        nc.sync.dma_start(out_list[:], offs4)

        wq_plane = sb.tile([P, K], U8, align_bytes=64)
        wq_codes = sb.tile([P, K], U32, align_bytes=64)
        nc.vector.tensor_copy(
            out=wq_plane[:].rearrange("p (j m) -> p m j", j=PLACES), in_=wq_plane_raw[:].rearrange("p (m j) -> p m j", j=PLACES)
        )
        dealt = wq_codes[:].rearrange("p (j m) -> p m j", j=PLACES)
        undealt = wq_codes_raw[:].rearrange("p (m j) -> p m j", j=PLACES)

        states_bf = sb.tile([P, Q * PLACES], BF16, align_bytes=64)
        states_codes = sb.tile([P, Q], U32, align_bytes=64)
        states_plane = sb.tile([P, Q], U8, align_bytes=64)
        row_halves = [slice(h * Q // 2, (h + 1) * Q // 2) for h in range(2)]
        for engine_copy, rows in zip((nc.vector.tensor_copy, nc.scalar.copy), row_halves):
            engine_copy(
                out=states_bf[:, PLACES * rows.start : PLACES * rows.stop].rearrange("p (q j) -> p q j", j=PLACES),
                in_=states_raw[:, :, rows].rearrange("p j q -> p q j"),
            )
        for rows in row_halves:
            nc.vector.quantize_mx(
                out=states_codes[:, rows].bitcast(FP8X4),
                scales=states_plane[:, rows],
                in_=states_bf[:, PLACES * rows.start : PLACES * rows.stop],
            )

        nc.scalar.copy(out=dealt[:, :DEAL_ON_SCALAR, :], in_=undealt[:, :DEAL_ON_SCALAR, :])
        nc.vector.tensor_copy(out=dealt[:, DEAL_ON_SCALAR:, :].bitcast(I32), in_=undealt[:, DEAL_ON_SCALAR:, :].bitcast(I32))

        qv_banks = [ps.tile([P, 2, Q], F32, name=f"qv_bank{pair}") for pair in range(PLACES // 2)]
        for j in range(PLACES):
            cols = slice(P * j, P * (j + 1))
            nc.tensor.matmul_mx(
                out=qv_banks[j // 2][:, j % 2, :],
                lhsT=wq_codes[:, cols].bitcast(FP8X4),
                lhsT_scale=wq_plane[:, cols],
                rhs=states_codes[:].bitcast(FP8X4),
                rhs_scale=states_plane[:],
                start=True,
                stop=True,
            )

        spans = [slice(first, last) for first, last in zip(SCORE_EDGES, SCORE_EDGES[1:])]
        banks = [ps.tile([P, cols.stop - cols.start], F32, name=f"score_bank{cols.start}") for cols in spans]
        for cols, bank in zip(spans, banks):
            nc.tensor.matmul_mx(
                out=bank[:],
                lhsT=states_codes[:].bitcast(FP8X4),
                lhsT_scale=states_plane[:],
                rhs=tags_codes[:, cols].bitcast(FP8X4),
                rhs_scale=tags_plane[:, cols],
                start=True,
                stop=False,
            )

        qv_bf = sb.tile([P, Q * PLACES], BF16, align_bytes=64)
        qv_codes = sb.tile([P, Q], U32, align_bytes=64)
        qv_plane = sb.tile([P, Q], U8, align_bytes=64)
        qv_places = qv_bf[:].rearrange("p (q j) -> p q j", j=PLACES)
        nc.vector.tensor_copy(out=qv_places[:, :, 0:2], in_=qv_banks[0][:].rearrange("p j q -> p q j"))
        nc.scalar.copy(out=qv_places[:, :, 2:4], in_=qv_banks[1][:].rearrange("p j q -> p q j"))
        nc.vector.quantize_mx(out=qv_codes[:].bitcast(FP8X4), scales=qv_plane[:], in_=qv_bf[:])

        a = sb.tile([P, T], F32, align_bytes=64)
        for b, (cols, bank) in enumerate(zip(spans, banks)):
            nc.tensor.matmul_mx(
                out=bank[:],
                lhsT=qv_codes[:].bitcast(FP8X4),
                lhsT_scale=qv_plane[:],
                rhs=keys_codes[:, 2 * cols.start : 2 * cols.stop].bitcast(FP4X4),
                rhs_scale=keys_plane[:, cols],
                start=False,
                stop=True,
            )
            if b % 2 == 1:
                nc.scalar.copy(out=a[:, cols], in_=bank[:])
            else:
                nc.vector.tensor_copy(out=a[:, cols], in_=bank[:])

        first, second = [slice(h * HALF // HEAD_ROWS, (h + 1) * HALF // HEAD_ROWS) for h in range(2)]
        gate_first = sb.tile([P, HALF], F32)
        gate_second = sb.tile([P, HALF], F32)
        passed_first = sb.tile([P, HALF], F32)
        nc.vector.tensor_copy(passed_first[:], a[:].indirect(pass_list[:, first]))
        for gate, half in ((gate_first, first), (gate_second, second)):
            nc.scalar.activation(gate[:], a[:].indirect(gate_list[:, half]), ACT.Sigmoid, bias=thr_col[:], scale=slope_col[:])
        passed_second = sb.tile([P, HALF], F32, tag="thr_then_passed")
        nc.scalar.activation(passed_second[:], a[:].indirect(pass_list[:, second]), ACT.Copy)

        for passed, gate, half in ((passed_first, gate_first, first), (passed_second, gate_second, second)):
            nc.vector.tensor_tensor(f1[:].indirect(place_list[:, half]), passed[:], gate[:], ALU.mult)

        cc = sb.tile([P, T], F32, align_bytes=64)
        nc.gpsimd.tensor_tensor(cc[:, ADD_ON_VECTOR:], a[:, ADD_ON_VECTOR:], f1[:, ADD_ON_VECTOR:], ALU.add)
        for span, bank in zip(spans, banks):
            if span.start < ADD_ON_VECTOR:
                cols = slice(span.start, min(span.stop, ADD_ON_VECTOR))
                nc.vector.tensor_tensor(cc[:, cols], bank[:, : cols.stop - cols.start], f1[:, cols], ALU.add)

        result_first = sb.tile([P, HALF], F32)
        result_second = sb.tile([P, HALF], F32)
        nc.vector.tensor_copy(result_first[:], cc[:].indirect(out_list[:, first]))
        nc.scalar.activation(result_second[:], cc[:].indirect(out_list[:, second]), ACT.Copy)
        nc.sync.dma_start(out=out[:, :HALF], in_=result_first[:])
        nc.scalar.dma_start(out=out[:, HALF:], in_=result_second[:])
